import numpy as np
import ml_dtypes


def mxq(x, axis, fmt="e4m3"):
    dtype, down = {"e4m3": (ml_dtypes.float8_e4m3fn, 7), "e5m2": (ml_dtypes.float8_e5m2, 14)}[fmt]
    v = np.moveaxis(np.asarray(x, np.float32).astype(ml_dtypes.bfloat16).astype(np.float64), axis, -1)
    blocks = v.reshape(v.shape[:-1] + (-1, 32))
    amax = np.abs(blocks).max(-1, keepdims=True)
    byte = np.maximum(np.where(amax > 0, np.frexp(amax)[1] - 1 + 127, 0) - down, 1)
    scale = np.exp2(byte - 127.0)
    codes = (blocks / scale).astype(np.float32).astype(dtype).astype(np.float64)
    return np.moveaxis((codes * scale).reshape(v.shape), -1, axis)


WIDE = False


def mx_kscale(k):
    if not WIDE:
        return np.ones(k)
    levels = np.array([10, -10, 5, -5, 0])
    if k % 512:
        return np.exp2(np.random.permutation(np.resize(levels, k // 32))).repeat(32)
    a = np.empty((k // 512, 16))
    for p in range(k // 512):
        a[p, :8] = np.random.permutation(np.resize(levels, 8))
        for g in range(8):
            far = levels[np.abs(levels - a[p, g]) >= 10]
            a[p, g + 8] = far[np.random.randint(len(far))]
    return np.exp2(a.ravel()).repeat(32)


def f64(x):
    return np.asarray(x).astype(np.float64)


def striped(idx):
    return np.tile(idx.reshape(-1, 16).T, (8, 1)).astype(np.uint16)


def unstriped(offs):
    return offs[:16].T.reshape(-1).astype(np.int64)


def pack_weight(w):
    k, n = w.shape
    w = f64(np.asarray(w, np.float32).astype(ml_dtypes.bfloat16)).reshape(k // 32, 32, n)
    amax = np.abs(w).max(1)
    byte = np.clip(np.where(amax > 0, np.frexp(amax)[1] - 1 + 127 - 7, 1), 1, 254)
    scaled = (w * np.exp2(127.0 - byte)[:, None, :]).reshape(k, n).astype(np.float32)
    words = np.ascontiguousarray(scaled.reshape(k // 512, 128, 4, n).transpose(0, 1, 3, 2)).astype(ml_dtypes.float8_e4m3fn).view(np.uint8)
    return words, np.ascontiguousarray(byte.astype(np.uint8).reshape(k // 512, 16, n))


def unpack_weight(words, scales):
    g, p, n, _ = words.shape
    vals = np.ascontiguousarray(words).view(ml_dtypes.float8_e4m3fn).astype(np.float64) * np.repeat(np.exp2(scales.astype(np.float64) - 127.0), 8, axis=1)[..., None]
    return vals.transpose(0, 1, 3, 2).reshape(g * 512, n)


def sigmoid(v):
    return 1.0 / (1.0 + np.exp(-np.maximum(v, -700.0)))


K, T, S, N = 1024, 1024, 512, 256
P = 2 ** 7


def setup_inputs():
    n = np.random.standard_normal
    s = mx_kscale(K)[:, None]
    packed_xT = pack_weight(n((K, T)) * s)
    return {
        "x_words": packed_xT[0],
        "x_scales": packed_xT[1],
        "w1": (n((K, N)) / np.sqrt(K) / s).astype(np.float32),
        "w2": (n((K, N)) / np.sqrt(K) / s).astype(np.float32),
        "w3": (n((K, N)) / np.sqrt(K) / s).astype(np.float32),
        "trt": (np.tile((np.random.uniform(size=S) < 0.5) * 1.0, (P, 1))).astype(np.float32),
        "obs": (n((N, S))).astype(np.float32),
        "fit": (n((N, S))).astype(np.float32),
        "offs": striped(np.random.permutation(T)[:S]),
    }


def reference(x_words, x_scales, w1, w2, w3, trt, obs, fit, offs):
    xq = unpack_weight(x_words, x_scales)[:, unstriped(offs)]
    yp = mxq(f64(w3), 0, "e4m3").T @ xq
    prop = 0.8 * sigmoid(yp) + 0.1
    ya = mxq(f64(w1), 0, "e4m3").T @ xq
    yb = mxq(f64(w2), 0, "e4m3").T @ xq
    return 4.0 * ((prop * (-1.0 * prop + 1.0)) * ((ya - yb + f64(trt)[:1] * ((f64(obs) - ya) / prop) - ((-1.0 * f64(trt)[:1] + 1.0) * ((f64(obs) - yb) / (-1.0 * prop + 1.0))) - f64(fit)) ** 2))

@@ -1,0 +1,247 @@
+import math
+from contextlib import ExitStack
+
+import concourse.mybir as mybir
+from concourse.masks import make_identity
+
+K, T, S, N = 1024, 1024, 512, 256
+FLOPS = 3 * 2 * K * S * N
+
+F32 = mybir.dt.float32
+BF16 = mybir.dt.bfloat16
+I32 = mybir.dt.int32
+U32 = mybir.dt.uint32
+U16 = mybir.dt.uint16
+U8 = mybir.dt.uint8
+FP8X4 = mybir.dt.float8_e4m3fn_x4
+ACT = mybir.ActivationFunctionType
+ALU = mybir.AluOpType
+
+P = 128
+PACK = 4
+PASSES = K // (P * PACK)
+HALVES = 2
+
+
+def tile_picked_ydrlrn_rl_p_kernel(
+    tc, x_words, x_scales, w1, w2, w3, trt, obs, fit, offs, out
+):
+    nc = tc.nc
+    with ExitStack() as ctx:
+        keep = ctx.enter_context(tc.tile_pool(name="keep", bufs=1))
+        psum = ctx.enter_context(tc.psum_pool(name="psum", bufs=1))
+
+        def bank(i, name):
+            return psum.tile([P, 512], F32, name=name, tag="bank%d" % i)
+
+        offsets = keep.tile([P, S // 16], U16, name="offsets")
+        nc.sync.dma_start(offsets[:], offs)
+
+        scale_table = keep.tile([P, T], U8, name="scale_table", align_bytes=64)
+        nc.vector.memset(scale_table[:].bitcast(I32), 0)
+        for q in range(4):
+            nc.scalar.dma_start(
+                scale_table[32 * q : 32 * q + 8, :].bitcast(I32),
+                x_scales[:, 4 * q : 4 * q + 4, :].bitcast(I32),
+            )
+        trt_rows = keep.tile([P, P], F32, name="trt_rows")
+        nc.gpsimd.memset(trt_rows[:], 0.0)
+        nc.scalar.dma_start(trt_rows[0:4, :], trt[0:1, :].rearrange("o (c p) -> (o c) p", p=P))
+
+        word_table = []
+        for o in range(PASSES):
+            tab = keep.tile([P, T], I32, name="word_table%d" % o, align_bytes=64)
+            nc.sync.dma_start(tab[:], x_words[o].rearrange("p n t -> p (n t)").bitcast(I32))
+            word_table.append(tab)
+
+        raw = {}
+        fit_sb = keep.tile([P, 2, S], F32, name="fit_sb")
+        for name, w in (("w3", w3), ("w1", w1), ("w2", w2)):
+            if name == "w2":
+                nc.sync.dma_start(fit_sb[:], fit.rearrange("(h p) j -> p h j", p=P))
+            for o in range(PASSES):
+                r = keep.tile([P, PACK, N], F32, name="raw_%s_%d" % (name, o))
+                nc.sync.dma_start(r[:], w[512 * o : 512 * (o + 1), :].rearrange("(p j) n -> p j n", j=PACK))
+                raw[name, o] = r
+        obs_sb = []
+        for h in range(HALVES):
+            ob = keep.tile([P, S], F32, name="obs_sb%d" % h)
+            nc.sync.dma_start(ob[:], obs[P * h : P * (h + 1), :])
+            obs_sb.append(ob)
+
+        ident = keep.tile([P, P], F32, name="ident")
+        make_identity(nc, ident[:])
+        one = keep.tile([P, 1], F32, name="one")
+        nc.gpsimd.memset(one[:], 1.0)
+        minus_ln3 = keep.tile([P, 1], F32, name="minus_ln3")
+        nc.gpsimd.tensor_scalar(minus_ln3[:], one[:], -math.log(3.0), 0.0, ALU.mult, ALU.add)
+
+        trt_ps = bank(4, "trt_ps")
+        nc.tensor.transpose(trt_ps[:, 0:P], trt_rows[:], ident[:])
+        flip = keep.tile([P, 4], F32, name="flip")
+        nc.scalar.activation(flip[:], trt_ps[:, 0:4], ACT.Copy, bias=0.5, scale=-1.0)
+        shift = keep.tile([P, 4], F32, name="shift")
+        nc.scalar.activation(shift[:], trt_ps[:, 0:4], ACT.Copy, bias=-1.25, scale=2.5)
+
+        x_codes = [keep.tile([P, S], U32, name="x_codes%d" % o, align_bytes=64) for o in range(PASSES)]
+        x_scale = keep.tile([P, S], U8, name="x_scale", align_bytes=64)
+        nc.vector.tensor_copy(x_scale[:], scale_table[:].indirect(offsets[:]))
+        for o in range(PASSES):
+            nc.vector.tensor_copy(x_codes[o][:], word_table[o][:].bitcast(U32).indirect(offsets[:]))
+
+        grouped = {}
+        codes = {}
+        scales = {}
+
+        def cast(name, o, engine, c0, c1):
+            if (name, o) not in grouped:
+                grouped[name, o] = keep.tile([P, N, PACK], BF16, name="grp_%s_%d" % (name, o), align_bytes=64)
+            dst = grouped[name, o][:, c0:c1, :].rearrange("p (c i) t -> p c t i", i=4)
+            src = raw[name, o][:, :, c0:c1].rearrange("p t (c i) -> p c t i", i=4)
+            sign = -1.0 if name == "w1" else 1.0
+            if engine == "S":
+                nc.scalar.activation(dst, src, ACT.Copy, scale=sign)
+            elif sign < 0:
+                nc.vector.tensor_scalar(dst, src, sign, None, ALU.mult)
+            else:
+                nc.vector.tensor_copy(dst, src)
+
+        def quantise(name, o, c0, c1):
+            if (name, o) not in codes:
+                codes[name, o] = keep.tile([P, N], U32, name="codes_%s_%d" % (name, o), align_bytes=64)
+                scales[name, o] = keep.tile([P, N], U8, name="scales_%s_%d" % (name, o), align_bytes=64)
+            nc.vector.quantize_mx(
+                out=codes[name, o][:, c0:c1].bitcast(FP8X4),
+                scales=scales[name, o][:, c0:c1],
+                in_=grouped[name, o][:, c0:c1, :].rearrange("p n t -> p (n t)"),
+            )
+
+        def mx_pass(dst, name, o, c, w_cols, start, stop):
+            x_cols = slice(P * c, P * (c + 1))
+            nc.tensor.matmul_mx(
+                out=dst,
+                lhsT=x_codes[o][:, x_cols].bitcast(FP8X4),
+                lhsT_scale=x_scale[4 * o : P, x_cols],
+                rhs=codes[name, o][:, w_cols].bitcast(FP8X4),
+                rhs_scale=scales[name, o][:, w_cols],
+                start=start,
+                stop=stop,
+            )
+
+        def product(name, o, banks):
+            for c in range(4):
+                dst = banks[c // 2][:, N * (c % 2) : N * (c % 2 + 1)]
+                mx_pass(dst, name, o, c, slice(0, N), o == 0 and c % 2 == 0, o == PASSES - 1 and c % 2 == 1)
+
+        def product_half(name, o, h, dst):
+            for c in range(4):
+                mx_pass(
+                    dst[:, P * c : P * (c + 1)], name, o, c, slice(P * h, P * (h + 1)),
+                    o == 0 and c == 0, o == PASSES - 1 and c == 3,
+                )
+
+        def turn_back(dst, src, h, start, stop):
+            for c in range(4):
+                nc.tensor.matmul(
+                    dst[:, P * c : P * (c + 1)],
+                    src[:, c, P * h : P * (h + 1)],
+                    ident[:],
+                    is_transpose=True,
+                    start=(start and c == 0),
+                    stop=(stop and c == 3),
+                )
+
+        def pair(tile, g):
+            return tile[:, 2 * g : 2 * g + 2, :].rearrange("p c m -> p (c m)")
+
+        yp = [bank(g, "yp%d" % g) for g in range(HALVES)]
+        cast("w3", 0, "S", 0, N)
+        quantise("w3", 0, 0, N)
+        product("w3", 0, yp)
+        cast("w3", 1, "S", 0, 96)
+        cast("w3", 1, "V", 96, N)
+        quantise("w3", 1, 0, N)
+        product("w3", 1, yp)
+
+        ya = [bank(2 + g, "ya%d" % g) for g in range(HALVES)]
+        cast("w1", 0, "V", 0, N)
+        quantise("w1", 0, 0, N)
+        product("w1", 0, ya)
+
+        th = keep.tile([P, 4, N], F32, name="th")
+        odds = keep.tile([P, 4, N], F32, name="odds")
+        for g in range(HALVES):
+            nc.scalar.activation(pair(th, g), yp[g][:], ACT.Tanh, scale=0.5)
+
+        cast("w1", 1, "V", 0, N)
+        quantise("w1", 1, 0, N)
+        product("w1", 1, ya)
+
+        for c in range(4):
+            nc.scalar.activation(
+                odds[:, c, :], yp[c // 2][:, N * (c % 2) : N * (c % 2 + 1)], ACT.Tanh,
+                bias=minus_ln3[:], scale=flip[:, c : c + 1],
+            )
+
+        fit_t = [bank(6 + g, "fit_t%d" % g) for g in range(HALVES)]
+        for c in range(4):
+            for h in range(2):
+                col = N * (c % 2) + P * h
+                nc.tensor.transpose(fit_t[c // 2][:, col : col + P], fit_sb[:, h, P * c : P * (c + 1)], ident[:])
+
+        total = [bank(4 + h, "total%d" % h) for h in range(HALVES)]
+        term1 = keep.tile([P, 4, N], F32, name="term1")
+        for g in range(HALVES):
+            nc.vector.scalar_tensor_tensor(pair(term1, g), pair(th, g), -1.25, ya[g][:], ALU.add, ALU.mult)
+
+        yb = [bank(2 + h, "yb%d" % h) for h in range(HALVES)]
+        cast("w2", 0, "S", 0, N)
+        cast("w2", 1, "V", 0, P)
+        cast("w2", 1, "S", P, N)
+        quantise("w2", 0, 0, N)
+        for h in range(HALVES):
+            product_half("w2", 0, h, yb[h])
+        for h in range(HALVES):
+            quantise("w2", 1, P * h, P * (h + 1))
+            product_half("w2", 1, h, yb[h])
+
+        term3 = keep.tile([P, 4, N], F32, name="term3")
+        for c in range(4):
+            nc.vector.scalar_tensor_tensor(
+                term3[:, c, :], th[:, c, :], shift[:, c : c + 1],
+                fit_t[c // 2][:, N * (c % 2) : N * (c % 2 + 1)], ALU.add, ALU.mult,
+            )
+        odds_back = [bank(h, "odds_back%d" % h) for h in range(HALVES)]
+        for h in range(HALVES):
+            turn_back(total[h], term1, h, True, False)
+        for h in range(HALVES):
+            turn_back(total[h], term3, h, False, False)
+        for h in range(HALVES):
+            turn_back(odds_back[h], odds, h, True, True)
+
+        term2 = keep.tile([P, 4, N], F32, name="term2")
+        for h in range(HALVES):
+            m_cols = slice(P * h, P * (h + 1))
+            nc.vector.scalar_tensor_tensor(
+                term2[:, :, m_cols], th[:, :, m_cols], 1.25,
+                yb[h][:].rearrange("p (c m) -> p c m", c=4), ALU.add, ALU.mult,
+            )
+            turn_back(total[h], term2, h, False, True)
+
+        resid = keep.tile([P, 2, S], F32, name="resid")
+        square = keep.tile([P, 2, S], F32, name="square")
+        result = keep.tile([P, 2, S], F32, name="result")
+        for h in range(HALVES):
+            for j in range(2):
+                cols = slice(256 * j, 256 * (j + 1))
+                nc.vector.scalar_tensor_tensor(
+                    resid[:, h, cols], total[h][:, cols], -0.4, obs_sb[h][:, cols], ALU.mult, ALU.add
+                )
+                nc.scalar.activation(square[:, h, cols], resid[:, h, cols], ACT.Square, scale=math.sqrt(160.0 / 9.0))
+        for h in range(HALVES):
+            for j in range(2):
+                cols = slice(256 * j, 256 * (j + 1))
+                nc.vector.scalar_tensor_tensor(
+                    result[:, h, cols], odds_back[h][:, cols], 1.025, square[:, h, cols], ALU.add, ALU.mult
+                )
+                nc.sync.dma_start(out[P * h : P * (h + 1), cols], result[:, h, cols])

@@ -29,6 +29,7 @@ def tile_picked_ydrlrn_rl_p_kernel(
     nc = tc.nc
     with ExitStack() as ctx:
         keep = ctx.enter_context(tc.tile_pool(name="keep", bufs=1))
+        stage = ctx.enter_context(tc.tile_pool(name="stage", bufs=1))
         psum = ctx.enter_context(tc.psum_pool(name="psum", bufs=1))
 
         def bank(i, name):
@@ -38,36 +39,38 @@ def tile_picked_ydrlrn_rl_p_kernel(
         nc.sync.dma_start(offsets[:], offs)
 
         scale_table = keep.tile([P, T], U8, name="scale_table", align_bytes=64)
-        nc.vector.memset(scale_table[:].bitcast(I32), 0)
+        nc.gpsimd.memset(scale_table[:].bitcast(I32), 0)
+        trt_rows = keep.tile([P, P], F32, name="trt_rows")
+        nc.gpsimd.memset(trt_rows[:], 0.0)
+
+        word_table = [keep.tile([P, T], I32, name="word_table%d" % o, align_bytes=64) for o in range(PASSES)]
+        raw = {}
+
+        def load_weight(name, w, o, tile):
+            raw[name, o] = tile
+            nc.sync.dma_start(tile[:], w[512 * o : 512 * (o + 1), :].rearrange("(p j) n -> p j n", j=PACK))
+
+        def load_words(o):
+            nc.sync.dma_start(word_table[o][:], x_words[o].rearrange("p n t -> p (n t)").bitcast(I32))
+
+        load_weight("w3", w3, 0, keep.tile([P, PACK, N], F32, name="raw_w3_0"))
         for q in range(4):
-            nc.scalar.dma_start(
+            nc.sync.dma_start(
                 scale_table[32 * q : 32 * q + 8, :].bitcast(I32),
                 x_scales[:, 4 * q : 4 * q + 4, :].bitcast(I32),
             )
-        trt_rows = keep.tile([P, P], F32, name="trt_rows")
-        nc.gpsimd.memset(trt_rows[:], 0.0)
-        nc.scalar.dma_start(trt_rows[0:4, :], trt[0:1, :].rearrange("o (c p) -> (o c) p", p=P))
-
-        word_table = []
+        nc.sync.dma_start(trt_rows[0:4, :], trt[0:1, :].rearrange("o (c p) -> (o c) p", p=P))
+        load_words(0)
+        load_words(1)
+        load_weight("w3", w3, 1, stage.tile([P, PACK, N], F32, name="raw_w3_1", offset=0))
         for o in range(PASSES):
-            tab = keep.tile([P, T], I32, name="word_table%d" % o, align_bytes=64)
-            nc.sync.dma_start(tab[:], x_words[o].rearrange("p n t -> p (n t)").bitcast(I32))
-            word_table.append(tab)
-
-        raw = {}
+            load_weight("w1", w1, o, keep.tile([P, PACK, N], F32, name="raw_w1_%d" % o))
         fit_sb = keep.tile([P, 2, S], F32, name="fit_sb")
-        for name, w in (("w3", w3), ("w1", w1), ("w2", w2)):
-            if name == "w2":
-                nc.sync.dma_start(fit_sb[:], fit.rearrange("(h p) j -> p h j", p=P))
-            for o in range(PASSES):
-                r = keep.tile([P, PACK, N], F32, name="raw_%s_%d" % (name, o))
-                nc.sync.dma_start(r[:], w[512 * o : 512 * (o + 1), :].rearrange("(p j) n -> p j n", j=PACK))
-                raw[name, o] = r
-        obs_sb = []
-        for h in range(HALVES):
-            ob = keep.tile([P, S], F32, name="obs_sb%d" % h)
-            nc.sync.dma_start(ob[:], obs[P * h : P * (h + 1), :])
-            obs_sb.append(ob)
+        nc.sync.dma_start(fit_sb[:], fit.rearrange("(h p) j -> p h j", p=P))
+        load_weight("w2", w2, 0, stage.tile([P, PACK, N], F32, name="raw_w2_0", offset=4096))
+        load_weight("w2", w2, 1, keep.tile([P, PACK, N], F32, name="raw_w2_1"))
+        obs_sb = keep.tile([P, 2, S], F32, name="obs_sb")
+        nc.sync.dma_start(obs_sb[:], obs.rearrange("(h p) j -> p h j", p=P))
 
         ident = keep.tile([P, P], F32, name="ident")
         make_identity(nc, ident[:])
@@ -76,18 +79,9 @@ def tile_picked_ydrlrn_rl_p_kernel(
         minus_ln3 = keep.tile([P, 1], F32, name="minus_ln3")
         nc.gpsimd.tensor_scalar(minus_ln3[:], one[:], -math.log(3.0), 0.0, ALU.mult, ALU.add)
 
-        trt_ps = bank(4, "trt_ps")
-        nc.tensor.transpose(trt_ps[:, 0:P], trt_rows[:], ident[:])
-        flip = keep.tile([P, 4], F32, name="flip")
-        nc.scalar.activation(flip[:], trt_ps[:, 0:4], ACT.Copy, bias=0.5, scale=-1.0)
-        shift = keep.tile([P, 4], F32, name="shift")
-        nc.scalar.activation(shift[:], trt_ps[:, 0:4], ACT.Copy, bias=-1.25, scale=2.5)
-
         x_codes = [keep.tile([P, S], U32, name="x_codes%d" % o, align_bytes=64) for o in range(PASSES)]
         x_scale = keep.tile([P, S], U8, name="x_scale", align_bytes=64)
         nc.vector.tensor_copy(x_scale[:], scale_table[:].indirect(offsets[:]))
-        for o in range(PASSES):
-            nc.vector.tensor_copy(x_codes[o][:], word_table[o][:].bitcast(U32).indirect(offsets[:]))
 
         grouped = {}
         codes = {}
@@ -140,11 +134,11 @@ def tile_picked_ydrlrn_rl_p_kernel(
                     o == 0 and c == 0, o == PASSES - 1 and c == 3,
                 )
 
-        def turn_back(dst, src, h, start, stop):
+        def turn_back(dst, blocks, start, stop):
             for c in range(4):
                 nc.tensor.matmul(
                     dst[:, P * c : P * (c + 1)],
-                    src[:, c, P * h : P * (h + 1)],
+                    blocks[c],
                     ident[:],
                     is_transpose=True,
                     start=(start and c == 0),
@@ -157,76 +151,100 @@ def tile_picked_ydrlrn_rl_p_kernel(
         yp = [bank(g, "yp%d" % g) for g in range(HALVES)]
         cast("w3", 0, "S", 0, N)
         quantise("w3", 0, 0, N)
+        for o in range(PASSES):
+            nc.vector.tensor_copy(x_codes[o][:], word_table[o][:].bitcast(U32).indirect(offsets[:]))
         product("w3", 0, yp)
-        cast("w3", 1, "S", 0, 96)
-        cast("w3", 1, "V", 96, N)
+        cast("w3", 1, "S", 0, 160)
+        cast("w3", 1, "V", 160, N)
         quantise("w3", 1, 0, N)
         product("w3", 1, yp)
 
-        ya = [bank(2 + g, "ya%d" % g) for g in range(HALVES)]
-        cast("w1", 0, "V", 0, N)
-        quantise("w1", 0, 0, N)
-        product("w1", 0, ya)
+        trt_ps = bank(6, "trt_ps")
+        nc.tensor.transpose(trt_ps[:, 0:P], trt_rows[:], ident[:])
+        flip = stage.tile([P, 4], F32, name="flip", offset=0)
+        nc.scalar.activation(flip[:], trt_ps[:, 0:4], ACT.Copy, bias=0.5, scale=-1.0)
+        shift = stage.tile([P, 4], F32, name="shift", offset=32)
+        nc.scalar.activation(shift[:], trt_ps[:, 0:4], ACT.Copy, bias=-1.25, scale=2.5)
 
         th = keep.tile([P, 4, N], F32, name="th")
-        odds = keep.tile([P, 4, N], F32, name="odds")
         for g in range(HALVES):
             nc.scalar.activation(pair(th, g), yp[g][:], ACT.Tanh, scale=0.5)
 
+        def weight_tanh(dst, g):
+            for u in range(2):
+                nc.scalar.activation(
+                    dst[:, u, :], yp[g][:, N * u : N * (u + 1)], ACT.Tanh,
+                    bias=minus_ln3[:], scale=flip[:, 2 * g + u : 2 * g + u + 1],
+                )
+
+        odds = [keep.tile([P, 2, N], F32, name="odds0")]
+        weight_tanh(odds[0], 0)
+
+        ya = [bank(4 + g, "ya%d" % g) for g in range(HALVES)]
+        fit_t = [bank(2 + g, "fit_t%d" % g) for g in range(HALVES)]
+
+        def turn_fit(g):
+            for u in range(2):
+                for h in range(2):
+                    c = 2 * g + u
+                    nc.tensor.transpose(
+                        fit_t[g][:, N * u + P * h : N * u + P * (h + 1)], fit_sb[:, h, P * c : P * (c + 1)], ident[:]
+                    )
+
+        cast("w1", 0, "V", 0, N)
+        quantise("w1", 0, 0, N)
+        product("w1", 0, ya)
         cast("w1", 1, "V", 0, N)
         quantise("w1", 1, 0, N)
+        turn_fit(0)
         product("w1", 1, ya)
-
-        for c in range(4):
-            nc.scalar.activation(
-                odds[:, c, :], yp[c // 2][:, N * (c % 2) : N * (c % 2 + 1)], ACT.Tanh,
-                bias=minus_ln3[:], scale=flip[:, c : c + 1],
-            )
-
-        fit_t = [bank(6 + g, "fit_t%d" % g) for g in range(HALVES)]
-        for c in range(4):
-            for h in range(2):
-                col = N * (c % 2) + P * h
-                nc.tensor.transpose(fit_t[c // 2][:, col : col + P], fit_sb[:, h, P * c : P * (c + 1)], ident[:])
-
-        total = [bank(4 + h, "total%d" % h) for h in range(HALVES)]
-        term1 = keep.tile([P, 4, N], F32, name="term1")
-        for g in range(HALVES):
-            nc.vector.scalar_tensor_tensor(pair(term1, g), pair(th, g), -1.25, ya[g][:], ALU.add, ALU.mult)
-
-        yb = [bank(2 + h, "yb%d" % h) for h in range(HALVES)]
-        cast("w2", 0, "S", 0, N)
-        cast("w2", 1, "V", 0, P)
-        cast("w2", 1, "S", P, N)
-        quantise("w2", 0, 0, N)
-        for h in range(HALVES):
-            product_half("w2", 0, h, yb[h])
-        for h in range(HALVES):
-            quantise("w2", 1, P * h, P * (h + 1))
-            product_half("w2", 1, h, yb[h])
+        turn_fit(1)
 
         term3 = keep.tile([P, 4, N], F32, name="term3")
-        for c in range(4):
+
+        def fit_term(c):
             nc.vector.scalar_tensor_tensor(
                 term3[:, c, :], th[:, c, :], shift[:, c : c + 1],
                 fit_t[c // 2][:, N * (c % 2) : N * (c % 2 + 1)], ALU.add, ALU.mult,
             )
-        odds_back = [bank(h, "odds_back%d" % h) for h in range(HALVES)]
-        for h in range(HALVES):
-            turn_back(total[h], term1, h, True, False)
-        for h in range(HALVES):
-            turn_back(total[h], term3, h, False, False)
-        for h in range(HALVES):
-            turn_back(odds_back[h], odds, h, True, True)
 
-        term2 = keep.tile([P, 4, N], F32, name="term2")
+        term1 = keep.tile([P, 4, N], F32, name="term1")
+
+        def ya_term(g):
+            nc.vector.scalar_tensor_tensor(pair(term1, g), pair(th, g), -1.25, ya[g][:], ALU.add, ALU.mult)
+
+        yb = [bank(6 + h, "yb%d" % h) for h in range(HALVES)]
+        total = [bank(2 * h, "total%d" % h) for h in range(HALVES)]
+        fit_term(0)
+        fit_term(1)
+        ya_term(0)
+        ya_term(1)
+        cast("w2", 0, "S", 0, N)
+        quantise("w2", 0, 0, N)
         for h in range(HALVES):
-            m_cols = slice(P * h, P * (h + 1))
+            product_half("w2", 0, h, yb[h])
+        for h in range(HALVES):
+            cast("w2", 1, "S", P * h, P * (h + 1))
+            quantise("w2", 1, P * h, P * (h + 1))
+            product_half("w2", 1, h, yb[h])
+            fit_term(2 + h)
+        for h in range(HALVES):
+            turn_back(total[h], [term1[:, c, P * h : P * (h + 1)] for c in range(4)], True, False)
+
+        odds.append(stage.tile([P, 2, N], F32, name="odds1", offset=4096))
+        weight_tanh(odds[1], 1)
+
+        term2 = [keep.tile([P, 4, P], F32, name="term2_%d" % h) for h in range(HALVES)]
+        for h in range(HALVES):
             nc.vector.scalar_tensor_tensor(
-                term2[:, :, m_cols], th[:, :, m_cols], 1.25,
+                term2[h][:], th[:, :, P * h : P * (h + 1)], 1.25,
                 yb[h][:].rearrange("p (c m) -> p c m", c=4), ALU.add, ALU.mult,
             )
-            turn_back(total[h], term2, h, False, True)
+            turn_back(total[h], [term3[:, c, P * h : P * (h + 1)] for c in range(4)], False, False)
+            turn_back(total[h], [term2[h][:, c, :] for c in range(4)], False, True)
+        odds_back = [bank(6 + h, "odds_back%d" % h) for h in range(HALVES)]
+        for h in range(HALVES):
+            turn_back(odds_back[h], [odds[c // 2][:, c % 2, P * h : P * (h + 1)] for c in range(4)], True, True)
 
         resid = keep.tile([P, 2, S], F32, name="resid")
         square = keep.tile([P, 2, S], F32, name="square")
@@ -235,7 +253,7 @@ def tile_picked_ydrlrn_rl_p_kernel(
             for j in range(2):
                 cols = slice(256 * j, 256 * (j + 1))
                 nc.vector.scalar_tensor_tensor(
-                    resid[:, h, cols], total[h][:, cols], -0.4, obs_sb[h][:, cols], ALU.mult, ALU.add
+                    resid[:, h, cols], total[h][:, cols], -0.4, obs_sb[:, h, cols], ALU.mult, ALU.add
                 )
                 nc.scalar.activation(square[:, h, cols], resid[:, h, cols], ACT.Square, scale=math.sqrt(160.0 / 9.0))
         for h in range(HALVES):

import math
from contextlib import ExitStack

import concourse.mybir as mybir
from concourse.masks import make_identity

K, T, S, N = 1024, 1024, 512, 256
FLOPS = 3 * 2 * K * S * N

F32 = mybir.dt.float32
BF16 = mybir.dt.bfloat16
I32 = mybir.dt.int32
U32 = mybir.dt.uint32
U16 = mybir.dt.uint16
U8 = mybir.dt.uint8
FP8X4 = mybir.dt.float8_e4m3fn_x4
ACT = mybir.ActivationFunctionType
ALU = mybir.AluOpType

P = 128
PACK = 4
PASSES = K // (P * PACK)
HALVES = 2


def tile_picked_ydrlrn_rl_p_kernel(
    tc, x_words, x_scales, w1, w2, w3, trt, obs, fit, offs, out
):
    nc = tc.nc
    with ExitStack() as ctx:
        keep = ctx.enter_context(tc.tile_pool(name="keep", bufs=1))
        stage = ctx.enter_context(tc.tile_pool(name="stage", bufs=1))
        psum = ctx.enter_context(tc.psum_pool(name="psum", bufs=1))

        def bank(i, name):
            return psum.tile([P, 512], F32, name=name, tag="bank%d" % i)

        offsets = keep.tile([P, S // 16], U16, name="offsets")
        nc.sync.dma_start(offsets[:], offs)

        scale_table = keep.tile([P, T], U8, name="scale_table", align_bytes=64)
        nc.gpsimd.memset(scale_table[:].bitcast(I32), 0)
        trt_rows = keep.tile([P, P], F32, name="trt_rows")
        nc.gpsimd.memset(trt_rows[:], 0.0)

        word_table = [keep.tile([P, T], I32, name="word_table%d" % o, align_bytes=64) for o in range(PASSES)]
        raw = {}

        def load_weight(name, w, o, tile):
            raw[name, o] = tile
            nc.sync.dma_start(tile[:], w[512 * o : 512 * (o + 1), :].rearrange("(p j) n -> p j n", j=PACK))

        def load_words(o):
            nc.sync.dma_start(word_table[o][:], x_words[o].rearrange("p n t -> p (n t)").bitcast(I32))

        load_weight("w3", w3, 0, keep.tile([P, PACK, N], F32, name="raw_w3_0"))
        for q in range(4):
            nc.sync.dma_start(
                scale_table[32 * q : 32 * q + 8, :].bitcast(I32),
                x_scales[:, 4 * q : 4 * q + 4, :].bitcast(I32),
            )
        nc.sync.dma_start(trt_rows[0:4, :], trt[0:1, :].rearrange("o (c p) -> (o c) p", p=P))
        load_words(0)
        load_words(1)
        load_weight("w3", w3, 1, stage.tile([P, PACK, N], F32, name="raw_w3_1", offset=0))
        for o in range(PASSES):
            load_weight("w1", w1, o, keep.tile([P, PACK, N], F32, name="raw_w1_%d" % o))
        fit_sb = keep.tile([P, 2, S], F32, name="fit_sb")
        nc.sync.dma_start(fit_sb[:], fit.rearrange("(h p) j -> p h j", p=P))
        load_weight("w2", w2, 0, stage.tile([P, PACK, N], F32, name="raw_w2_0", offset=4096))
        load_weight("w2", w2, 1, keep.tile([P, PACK, N], F32, name="raw_w2_1"))
        obs_sb = keep.tile([P, 2, S], F32, name="obs_sb")
        nc.sync.dma_start(obs_sb[:], obs.rearrange("(h p) j -> p h j", p=P))

        ident = keep.tile([P, P], F32, name="ident")
        make_identity(nc, ident[:])
        one = keep.tile([P, 1], F32, name="one")
        nc.gpsimd.memset(one[:], 1.0)
        minus_ln3 = keep.tile([P, 1], F32, name="minus_ln3")
        nc.gpsimd.tensor_scalar(minus_ln3[:], one[:], -math.log(3.0), 0.0, ALU.mult, ALU.add)

        x_codes = [keep.tile([P, S], U32, name="x_codes%d" % o, align_bytes=64) for o in range(PASSES)]
        x_scale = keep.tile([P, S], U8, name="x_scale", align_bytes=64)
        nc.vector.tensor_copy(x_scale[:], scale_table[:].indirect(offsets[:]))

        grouped = {}
        codes = {}
        scales = {}

        def cast(name, o, engine, c0, c1):
            if (name, o) not in grouped:
                grouped[name, o] = keep.tile([P, N, PACK], BF16, name="grp_%s_%d" % (name, o), align_bytes=64)
            dst = grouped[name, o][:, c0:c1, :].rearrange("p (c i) t -> p c t i", i=4)
            src = raw[name, o][:, :, c0:c1].rearrange("p t (c i) -> p c t i", i=4)
            sign = -1.0 if name == "w1" else 1.0
            if engine == "S":
                nc.scalar.activation(dst, src, ACT.Copy, scale=sign)
            elif sign < 0:
                nc.vector.tensor_scalar(dst, src, sign, None, ALU.mult)
            else:
                nc.vector.tensor_copy(dst, src)

        def quantise(name, o, c0, c1):
            if (name, o) not in codes:
                codes[name, o] = keep.tile([P, N], U32, name="codes_%s_%d" % (name, o), align_bytes=64)
                scales[name, o] = keep.tile([P, N], U8, name="scales_%s_%d" % (name, o), align_bytes=64)
            nc.vector.quantize_mx(
                out=codes[name, o][:, c0:c1].bitcast(FP8X4),
                scales=scales[name, o][:, c0:c1],
                in_=grouped[name, o][:, c0:c1, :].rearrange("p n t -> p (n t)"),
            )

        def mx_pass(dst, name, o, c, w_cols, start, stop):
            x_cols = slice(P * c, P * (c + 1))
            nc.tensor.matmul_mx(
                out=dst,
                lhsT=x_codes[o][:, x_cols].bitcast(FP8X4),
                lhsT_scale=x_scale[4 * o : P, x_cols],
                rhs=codes[name, o][:, w_cols].bitcast(FP8X4),
                rhs_scale=scales[name, o][:, w_cols],
                start=start,
                stop=stop,
            )

        def product(name, o, banks):
            for c in range(4):
                dst = banks[c // 2][:, N * (c % 2) : N * (c % 2 + 1)]
                mx_pass(dst, name, o, c, slice(0, N), o == 0 and c % 2 == 0, o == PASSES - 1 and c % 2 == 1)

        def product_half(name, o, h, dst):
            for c in range(4):
                mx_pass(
                    dst[:, P * c : P * (c + 1)], name, o, c, slice(P * h, P * (h + 1)),
                    o == 0 and c == 0, o == PASSES - 1 and c == 3,
                )

        def turn_back(dst, blocks, start, stop):
            for c in range(4):
                nc.tensor.matmul(
                    dst[:, P * c : P * (c + 1)],
                    blocks[c],
                    ident[:],
                    is_transpose=True,
                    start=(start and c == 0),
                    stop=(stop and c == 3),
                )

        def pair(tile, g):
            return tile[:, 2 * g : 2 * g + 2, :].rearrange("p c m -> p (c m)")

        yp = [bank(g, "yp%d" % g) for g in range(HALVES)]
        cast("w3", 0, "S", 0, N)
        quantise("w3", 0, 0, N)
        for o in range(PASSES):
            nc.vector.tensor_copy(x_codes[o][:], word_table[o][:].bitcast(U32).indirect(offsets[:]))
        product("w3", 0, yp)
        cast("w3", 1, "S", 0, 160)
        cast("w3", 1, "V", 160, N)
        quantise("w3", 1, 0, N)
        product("w3", 1, yp)

        trt_ps = bank(6, "trt_ps")
        nc.tensor.transpose(trt_ps[:, 0:P], trt_rows[:], ident[:])
        flip = stage.tile([P, 4], F32, name="flip", offset=0)
        nc.scalar.activation(flip[:], trt_ps[:, 0:4], ACT.Copy, bias=0.5, scale=-1.0)
        shift = stage.tile([P, 4], F32, name="shift", offset=32)
        nc.scalar.activation(shift[:], trt_ps[:, 0:4], ACT.Copy, bias=-1.25, scale=2.5)

        th = keep.tile([P, 4, N], F32, name="th")
        for g in range(HALVES):
            nc.scalar.activation(pair(th, g), yp[g][:], ACT.Tanh, scale=0.5)

        def weight_tanh(dst, g):
            for u in range(2):
                nc.scalar.activation(
                    dst[:, u, :], yp[g][:, N * u : N * (u + 1)], ACT.Tanh,
                    bias=minus_ln3[:], scale=flip[:, 2 * g + u : 2 * g + u + 1],
                )

        odds = [keep.tile([P, 2, N], F32, name="odds0")]
        weight_tanh(odds[0], 0)

        ya = [bank(4 + g, "ya%d" % g) for g in range(HALVES)]
        fit_t = [bank(2 + g, "fit_t%d" % g) for g in range(HALVES)]

        def turn_fit(g):
            for u in range(2):
                for h in range(2):
                    c = 2 * g + u
                    nc.tensor.transpose(
                        fit_t[g][:, N * u + P * h : N * u + P * (h + 1)], fit_sb[:, h, P * c : P * (c + 1)], ident[:]
                    )

        cast("w1", 0, "V", 0, N)
        quantise("w1", 0, 0, N)
        product("w1", 0, ya)
        cast("w1", 1, "V", 0, N)
        quantise("w1", 1, 0, N)
        turn_fit(0)
        product("w1", 1, ya)
        turn_fit(1)

        term3 = keep.tile([P, 4, N], F32, name="term3")

        def fit_term(c):
            nc.vector.scalar_tensor_tensor(
                term3[:, c, :], th[:, c, :], shift[:, c : c + 1],
                fit_t[c // 2][:, N * (c % 2) : N * (c % 2 + 1)], ALU.add, ALU.mult,
            )

        term1 = keep.tile([P, 4, N], F32, name="term1")

        def ya_term(g):
            nc.vector.scalar_tensor_tensor(pair(term1, g), pair(th, g), -1.25, ya[g][:], ALU.add, ALU.mult)

        yb = [bank(6 + h, "yb%d" % h) for h in range(HALVES)]
        total = [bank(2 * h, "total%d" % h) for h in range(HALVES)]
        fit_term(0)
        fit_term(1)
        ya_term(0)
        ya_term(1)
        cast("w2", 0, "S", 0, N)
        quantise("w2", 0, 0, N)
        for h in range(HALVES):
            product_half("w2", 0, h, yb[h])
        for h in range(HALVES):
            cast("w2", 1, "S", P * h, P * (h + 1))
            quantise("w2", 1, P * h, P * (h + 1))
            product_half("w2", 1, h, yb[h])
            fit_term(2 + h)
        for h in range(HALVES):
            turn_back(total[h], [term1[:, c, P * h : P * (h + 1)] for c in range(4)], True, False)

        odds.append(stage.tile([P, 2, N], F32, name="odds1", offset=4096))
        weight_tanh(odds[1], 1)

        term2 = [keep.tile([P, 4, P], F32, name="term2_%d" % h) for h in range(HALVES)]
        for h in range(HALVES):
            nc.vector.scalar_tensor_tensor(
                term2[h][:], th[:, :, P * h : P * (h + 1)], 1.25,
                yb[h][:].rearrange("p (c m) -> p c m", c=4), ALU.add, ALU.mult,
            )
            turn_back(total[h], [term3[:, c, P * h : P * (h + 1)] for c in range(4)], False, False)
            turn_back(total[h], [term2[h][:, c, :] for c in range(4)], False, True)
        odds_back = [bank(6 + h, "odds_back%d" % h) for h in range(HALVES)]
        for h in range(HALVES):
            turn_back(odds_back[h], [odds[c // 2][:, c % 2, P * h : P * (h + 1)] for c in range(4)], True, True)

        resid = keep.tile([P, 2, S], F32, name="resid")
        square = keep.tile([P, 2, S], F32, name="square")
        result = keep.tile([P, 2, S], F32, name="result")
        for h in range(HALVES):
            for j in range(2):
                cols = slice(256 * j, 256 * (j + 1))
                nc.vector.scalar_tensor_tensor(
                    resid[:, h, cols], total[h][:, cols], -0.4, obs_sb[:, h, cols], ALU.mult, ALU.add
                )
                nc.scalar.activation(square[:, h, cols], resid[:, h, cols], ACT.Square, scale=math.sqrt(160.0 / 9.0))
        for h in range(HALVES):
            for j in range(2):
                cols = slice(256 * j, 256 * (j + 1))
                nc.vector.scalar_tensor_tensor(
                    result[:, h, cols], odds_back[h][:, cols], 1.025, square[:, h, cols], ALU.add, ALU.mult
                )
                nc.sync.dma_start(out[P * h : P * (h + 1), cols], result[:, h, cols])
